import numpy as np
import ml_dtypes


def mxq(x, axis, fmt="e4m3"):
    dtype, down = {"e4m3": (ml_dtypes.float8_e4m3fn, 7), "e5m2": (ml_dtypes.float8_e5m2, 14)}[fmt]
    v = np.moveaxis(np.asarray(x, np.float32).astype(ml_dtypes.bfloat16).astype(np.float64), axis, -1)
    blocks = v.reshape(v.shape[:-1] + (-1, 32))
    amax = np.abs(blocks).max(-1, keepdims=True)
    byte = np.maximum(np.where(amax > 0, np.frexp(amax)[1] - 1 + 127, 0) - down, 1)
    scale = np.exp2(byte - 127.0)
    codes = (blocks / scale).astype(np.float32).astype(dtype).astype(np.float64)
    return np.moveaxis((codes * scale).reshape(v.shape), -1, axis)


WIDE = False


def mx_kscale(k):
    if not WIDE:
        return np.ones(k)
    levels = np.array([10, -10, 5, -5, 0])
    if k % 512:
        return np.exp2(np.random.permutation(np.resize(levels, k // 32))).repeat(32)
    a = np.empty((k // 512, 16))
    for p in range(k // 512):
        a[p, :8] = np.random.permutation(np.resize(levels, 8))
        for g in range(8):
            far = levels[np.abs(levels - a[p, g]) >= 10]
            a[p, g + 8] = far[np.random.randint(len(far))]
    return np.exp2(a.ravel()).repeat(32)


BF16 = ml_dtypes.bfloat16


def bf(x):
    return np.asarray(x, np.float32).astype(BF16)


def f64(x):
    return np.asarray(x).astype(np.float64)


E2M1 = np.array([0.0, 0.5, 1.0, 1.5, 2.0, 3.0, 4.0, 6.0, -0.0, -0.5, -1.0, -1.5, -2.0, -3.0, -4.0, -6.0])


def pack_weight(w, fmt):
    k, n = w.shape
    w = f64(bf(w)).reshape(k // 32, 32, n)
    amax = np.abs(w).max(1)
    if fmt == "e4m3":
        byte = np.frexp(amax)[1] - 1 + 127 - 7
    else:
        mant, ex = np.frexp(amax / 6.0)
        byte = np.where(mant > 0.5, ex, ex - 1) + 127
    byte = np.clip(np.where(amax > 0, byte, 1), 1, 254)
    scaled = (w * np.exp2(127.0 - byte)[:, None, :]).reshape(k, n).astype(np.float32)
    by_word = np.ascontiguousarray(scaled.reshape(k // 512, 128, 4, n).transpose(0, 1, 3, 2))
    if fmt == "e4m3":
        words = by_word.astype(ml_dtypes.float8_e4m3fn).view(np.uint8)
    else:
        c = by_word.astype(ml_dtypes.float4_e2m1fn).view(np.uint8) & 0xF
        words = c[..., 0::2] | (c[..., 1::2] << 4)
    return np.ascontiguousarray(words), np.ascontiguousarray(byte.astype(np.uint8).reshape(k // 512, 16, n))


def unpack_weight(words, scales, fmt):
    g, p, n, _ = words.shape
    if fmt == "e4m3":
        vals = np.ascontiguousarray(words).view(ml_dtypes.float8_e4m3fn).astype(np.float64)
    else:
        nib = np.empty((g, p, n, 4), np.uint8)
        nib[..., 0::2] = words & 0xF
        nib[..., 1::2] = words >> 4
        vals = E2M1[nib]
    vals = vals * np.repeat(np.exp2(scales.astype(np.float64) - 127.0), 8, axis=1)[..., None]
    return vals.transpose(0, 1, 3, 2).reshape(g * 512, n)
def pack4(w):
    words, scales = pack_weight(w, "e2m1")
    return words.reshape(words.shape[0], 128, -1), scales


def unpack4(words, scales):
    return unpack_weight(words.reshape(words.shape[0], 128, -1, 2), scales, "e2m1")


M, S, O = 1024, 2048, 1024

NU = 4.0
CLIP = 2.5


def setup_inputs():
    s, t = mx_kscale(S), mx_kscale(O)
    obs = np.random.standard_normal((S, O)) / np.sqrt(S) / s[:, None]
    gain = np.random.standard_normal((O, S)) / np.sqrt(O) / t[:, None]
    obs_words, obs_scales = pack4(obs)
    gain_words, gain_scales = pack_weight(gain, "e4m3")
    spread = np.random.uniform(0.5, 2.0, (M, 1))
    return {"x": bf(np.random.standard_normal((M, S))),
            "z": bf(np.random.standard_normal((M, O)) * spread),
            "decay": bf(0.9 + 0.05 * np.random.standard_normal(S)),
            "drift": bf(0.3 * np.random.standard_normal(S)),
            "unit": bf((1 + 0.1 * np.random.standard_normal(S)) * s),
            "obs_words": obs_words,
            "obs_scales": obs_scales,
            "obs_bias": bf(0.3 * np.random.standard_normal(O)),
            "rinv": bf(1 + 0.1 * np.random.standard_normal(O)),
            "trust": bf((1 + 0.1 * np.random.standard_normal(O)) * t),
            "gain_words": gain_words,
            "gain_scales": gain_scales}


def reference(x, z, decay, drift, unit, obs_words, obs_scales, obs_bias, rinv, trust, gain_words, gain_scales):
    xf = f64(x) * f64(decay) + f64(drift)
    y = mxq(xf * f64(unit), 1, "e4m3") @ unpack4(obs_words, obs_scales)
    u = (f64(z) - y - f64(obs_bias)) * f64(rinv)
    nis = np.mean(u * u, axis=1, keepdims=True)
    w = (NU + 1.0) / (NU + nis)
    e = np.minimum(np.maximum(u, -CLIP), CLIP) * f64(trust)
    c = mxq(e, 1, "e4m3") @ unpack_weight(gain_words, gain_scales, "e4m3")
    return xf + w * c, nis

@@ -1,0 +1,391 @@
+from contextlib import ExitStack
+
+import concourse.mybir as mybir
+from concourse.masks import make_identity
+
+M, S, O = 1024, 2048, 1024
+NU = 4.0
+CLIP = 2.5
+FLOPS = 2 * 2 * M * S * O
+
+F32 = mybir.dt.float32
+BF16 = mybir.dt.bfloat16
+I32 = mybir.dt.int32
+U32 = mybir.dt.uint32
+U8 = mybir.dt.uint8
+FP8X4 = mybir.dt.float8_e4m3fn_x4
+FP4X4 = mybir.dt.float4_e2m1fn_x4
+ACT = mybir.ActivationFunctionType
+ALU = mybir.AluOpType
+
+P = 128
+KP = 512
+NT = M // P
+GS = S // KP
+GO = O // KP
+
+
+def tile_robust_gain_update_f7_kernel(
+    tc, x, z, decay, drift, unit, obs_words, obs_scales, obs_bias, rinv, trust, gain_words, gain_scales, out_0, out_1
+):
+    nc = tc.nc
+    with ExitStack() as ctx:
+        keep = ctx.enter_context(tc.tile_pool(name="keep", bufs=1))
+        work = ctx.enter_context(tc.tile_pool(name="work", bufs=2))
+        psum = ctx.enter_context(tc.psum_pool(name="psum", bufs=1))
+        ctx.enter_context(tc.manual_schedule())
+
+        ident_f = keep.tile([P, P], F32, name="ident_f")
+        ident_b = keep.tile([P, P], BF16, name="ident_b")
+        ones_b = keep.tile([P, P], BF16, name="ones_b")
+        vec_rows = keep.tile([P, KP], BF16, name="vec_rows")
+        chan_rows = keep.tile([P, 3 * O + 16], BF16, name="chan_rows")
+        ident_rep = keep.tile([P, S], BF16, name="ident_rep")
+        hw = keep.tile([P, GS, 2 * O], U8, name="hw", align_bytes=64)
+        hs = keep.tile([P, GS, O], U8, name="hs", align_bytes=64)
+        gw = keep.tile([P, GO, 4 * S], U8, name="gw", align_bytes=64)
+        gs = keep.tile([P, GO, S], U8, name="gs", align_bytes=64)
+        x_sb = keep.tile([P, NT, S], BF16, name="x_sb")
+        z_sb = keep.tile([P, NT, O], BF16, name="z_sb")
+        xts = [keep.tile([P, S], BF16, name="xts%d" % i) for i in range(3)]
+        pv = keep.tile([P, 4, 12], F32, name="pv")
+        a_sb = keep.tile([P, 4, GS], F32, name="a_sb")
+        b_sb = keep.tile([P, 4, GS], F32, name="b_sb")
+        kcol = keep.tile([P, 1], F32, name="kcol")
+        decm = keep.tile([P, 4, GS], F32, name="decm")
+        dmat = keep.tile([P, GS, 4, P], BF16, name="dmat")
+        chan = keep.tile([P, 3 * O], BF16, name="chan")
+        dec16 = keep.tile([P, GS, 4], BF16, name="dec16")
+        xfix = keep.tile([P, NT, GS, 4], F32, name="xfix")
+        ssq = keep.tile([P, NT, 8], F32, name="ssq")
+        wden = keep.tile([P, NT, 8], F32, name="wden")
+        wgt = keep.tile([P, NT, 8], F32, name="wgt")
+        nis_all = keep.tile([P, P], F32, name="nis_all")
+        nis_t = keep.tile([NT, P], F32, name="nis_t")
+
+
+        make_identity(nc, ident_b[:])
+        make_identity(nc, ident_f[:])
+        nc.vector.memset(vec_rows[:], 0.0)
+        for i, v in enumerate((decay, drift, unit)):
+            nc.scalar.dma_start(out=vec_rows[4 * i : 4 * i + 4, :], in_=v.rearrange("(g r) -> g r", r=KP))
+        for hh in range(2):
+            nc.sync.dma_start(out=x_sb[:, 0, hh * 1024 : (hh + 1) * 1024], in_=x[0:P, hh * 1024 : (hh + 1) * 1024])
+        nc.vector.memset(hs[:].rearrange("p g n -> p (g n)").bitcast(I32), 0)
+        nc.vector.memset(ones_b[:], 1.0)
+        nc.vector.memset(chan_rows[:], 0.0)
+        nc.vector.memset(xts[0][:], 1.0)
+        nc.gpsimd.memset(xts[1][:], 1.0)
+        for i, v in enumerate((obs_bias, rinv, trust)):
+            nc.gpsimd.dma_start(out=chan_rows[0:1, i * O : (i + 1) * O], in_=v.rearrange("(o n) -> o n", o=1))
+        nc.gpsimd.dma_start(
+            out=chan_rows[0:1, 3 * O : 3 * O + 16].rearrange("o (g r) -> o g r", r=4),
+            in_=decay.rearrange("(o g r) -> o g r", o=1, r=KP)[:, :, KP - 4 : KP],
+        )
+        nc.gpsimd.memset(gs[:].rearrange("p g n -> p (g n)").bitcast(I32), 0)
+
+        hs_i = hs[:].rearrange("p g n -> p (g n)").bitcast(I32).rearrange("p (g n) -> p g n", g=GS)
+        hw_i = hw[:].rearrange("p g n -> p (g n)").bitcast(I32).rearrange("p (g n) -> p g n", g=GS)
+        gs_i = gs[:].rearrange("p g n -> p (g n)").bitcast(I32).rearrange("p (g n) -> p g n", g=GO)
+        gw_i = gw[:].rearrange("p g n -> p (g n)").bitcast(I32).rearrange("p (g n) -> p g n", g=GO)
+        obs_w = obs_words.bitcast(I32)
+        obs_s = obs_scales.bitcast(I32)
+        gain_w = gain_words.rearrange("g p n t -> g p (n t)").bitcast(I32)
+        gain_s = gain_scales.bitcast(I32)
+
+        def load_x(i):
+            nc.sync.dma_start(out=x_sb[:, i, :], in_=x[i * P : (i + 1) * P, :])
+
+        def load_z(i):
+            nc.sync.dma_start(out=z_sb[:, i, :], in_=z[i * P : (i + 1) * P, :])
+
+        pv_ps = psum.tile([P, 4, P], BF16, name="pv_ps", tag="et", bufs=1)
+        for t in range(4):
+            nc.tensor.transpose(pv_ps[:, t, :], vec_rows[:, t : KP : 4], ident_b[:])
+        nc.vector.tensor_copy(out=pv[:], in_=pv_ps[:, :, 0:12])
+        nc.vector.tensor_tensor(out=a_sb[:], in0=pv[:, :, 0:4], in1=pv[:, :, 8:12], op=ALU.mult)
+        nc.vector.tensor_tensor(out=b_sb[:], in0=pv[:, :, 4:8], in1=pv[:, :, 8:12], op=ALU.mult)
+        nc.vector.tensor_copy(
+            out=ident_rep[:].rearrange("p (g j t) -> p g j t", g=GS, t=4),
+            in_=ident_b[:].unsqueeze(1).unsqueeze(3).to_broadcast([P, GS, P, 4]),
+        )
+        nc.gpsimd.dma_start(out=ident_rep[P - 1 : P, :], in_=drift.rearrange("(o n) -> o n", o=1))
+        nc.gpsimd.tensor_scalar(
+            out=kcol[:], in0=ident_f[:, P - 1 : P], scalar1=-1.0, scalar2=1.0, op0=ALU.mult, op1=ALU.add
+        )
+        nc.gpsimd.tensor_scalar(
+            out=decm[:], in0=pv[:, :, 0:4], scalar1=kcol[:, 0:1], scalar2=ident_f[:, P - 1 : P], op0=ALU.mult, op1=ALU.add
+        )
+
+        for q in range(4):
+            nc.sync.dma_start(
+                out=hs_i[32 * q : 32 * q + 4, :, :], in_=obs_s[:, 4 * q : 4 * q + 4, :].rearrange("g r n -> r g n")
+            )
+        load_x(1)
+        for k in range(2):
+            nc.sync.dma_start(
+                out=hw_i[:, 2 * k : 2 * k + 2, :], in_=obs_w[2 * k : 2 * k + 2, :, :].rearrange("g p n -> p g n")
+            )
+        load_z(0)
+        load_x(2)
+        load_z(1)
+        for q in range(4):
+            nc.sync.dma_start(
+                out=gs_i[32 * q : 32 * q + 4, :, :], in_=gain_s[:, 4 * q : 4 * q + 4, :].rearrange("g r n -> r g n")
+            )
+        for g in range(GO):
+            nc.sync.dma_start(out=gw_i[:, g, :], in_=gain_w[g, :, :])
+        for i in range(2, NT):
+            load_z(i)
+            if i + 1 < NT:
+                load_x(i + 1)
+
+        def build_dmat(g):
+            for t in range(4):
+                nc.scalar.activation(
+                    out=dmat[:, g, t, :], in_=ident_rep[:].rearrange("p (g j t) -> p g j t", g=GS, t=4)[:, g, :, t],
+                    func=ACT.Copy, scale=decm[:, t, g : g + 1],
+                )
+
+        def channel_tables():
+            for k in range(3):
+                cb_ps = psum.tile([P, O], BF16, name="cb_ps", tag="acc", bufs=3)
+                for h in range(2):
+                    cols = slice(k * O + h * KP, k * O + (h + 1) * KP)
+                    nc.tensor.matmul(
+                        cb_ps[:, h * KP : (h + 1) * KP], lhsT=ones_b[:], rhs=chan_rows[:, cols], start=True, stop=True
+                    )
+                nc.vector.tensor_copy(out=chan[:, k * O : (k + 1) * O], in_=cb_ps[:])
+            d16_ps = psum.tile([P, 16], F32, name="d16_ps", tag="acc", bufs=3)
+            nc.tensor.matmul(d16_ps[:], lhsT=ones_b[:], rhs=chan_rows[:, 3 * O : 3 * O + 16], start=True, stop=True)
+            nc.vector.tensor_copy(out=dec16[:].rearrange("p g r -> p (g r)"), in_=d16_ps[:])
+
+        st = {}
+
+        def x_transposes(i, hh):
+            xt_ps = psum.tile([P, KP], F32, name="xt_ps", tag="xt%d" % hh, bufs=1)
+            words = x_sb[:, i, :].bitcast(F32)
+            for k in range(4):
+                g, u = 2 * hh + k // 2, k % 2
+                nc.tensor.transpose(
+                    xt_ps[:, k * P : (k + 1) * P], words[:, 256 * g + u : 256 * (g + 1) : 2], ident_f[:]
+                )
+            st["xt", i, hh] = xt_ps
+
+        def x_copy(i, hh):
+            nc.scalar.copy(
+                out=xts[i % 3][0 : P - 1, hh * 1024 : (hh + 1) * 1024].bitcast(F32),
+                in_=st["xt", i, hh][0 : P - 1, :],
+            )
+
+        def x_affine(i, hh):
+            if hh == 0:
+                st["v", i] = work.tile([P, 4, KP], BF16, name="v", bufs=2)
+            v = st["v", i]
+            pairs = st["xt", i, hh][:].bitcast(BF16).rearrange("p (k m e) -> p k m e", k=4, e=2)
+            for k in range(4):
+                g, u = 2 * hh + k // 2, k % 2
+                for e in range(2):
+                    t = 2 * u + e
+                    nc.scalar.activation(
+                        out=v[:, t, g * P : (g + 1) * P], in_=pairs[:, k, :, e], func=ACT.Identity,
+                        scale=a_sb[:, t, g : g + 1], bias=b_sb[:, t, g : g + 1],
+                    )
+
+        def x_interleave(i):
+            vi = work.tile([P, S], BF16, name="vi", bufs=2, align_bytes=64)
+            nc.vector.tensor_copy(
+                out=vi[:].rearrange("p (c i t) -> p c t i", i=4, t=4),
+                in_=st["v", i][:].rearrange("p t (c i) -> p c t i", i=4),
+            )
+            st["vi", i] = vi
+
+        def x_quantize(i):
+            vq = work.tile([P, KP], U32, name="vq", bufs=2, align_bytes=64)
+            vs = work.tile([P, KP], U8, name="vs", bufs=2, align_bytes=64)
+            nc.vector.quantize_mx(out=vq[:].bitcast(FP8X4), scales=vs[:], in_=st["vi", i][:])
+            st["vq", i] = (vq, vs)
+
+        def xf_products(i, g):
+            rows = xts[i % 3][:].rearrange("p (k m e) -> p k m e", k=8, e=2)
+            xf_ps = psum.tile([P, KP], F32, name="xf_ps", tag="acc", bufs=3)
+            for t in range(4):
+                nc.tensor.matmul(
+                    xf_ps[:, t * P : (t + 1) * P], lhsT=rows[:, 2 * g + t // 2, :, t % 2], rhs=dmat[:, g, t, :],
+                    start=True, stop=True,
+                )
+            st["xf_ps", i, g] = xf_ps
+
+        def xf_copy(i, g):
+            xf = work.tile([P, KP], F32, name="xf", tag="xf%d" % g, bufs=2)
+            nc.scalar.copy(
+                out=xf[:].rearrange("p (j t) -> p j t", t=4), in_=st["xf_ps", i, g][:].rearrange("p (t j) -> p j t", t=4)
+            )
+            nc.gpsimd.tensor_tensor(out=xf[:, KP - 4 : KP], in0=xf[:, KP - 4 : KP], in1=xfix[:, i, g, :], op=ALU.add)
+            st["xf", i, g] = xf
+
+        def z_bias(i):
+            zb = work.tile([P, O], F32, name="zb", bufs=2)
+            for h in range(2):
+                cols = slice(h * O // 2, (h + 1) * O // 2)
+                nc.gpsimd.tensor_tensor(out=zb[:, cols], in0=z_sb[:, i, cols], in1=chan[:, cols], op=ALU.subtract)
+            st["zb", i] = zb
+            nc.gpsimd.tensor_tensor(
+                out=xfix[:, i, :, :], in0=x_sb[:, i, :].rearrange("p (g r) -> p g r", g=GS)[:, :, KP - 4 : KP],
+                in1=dec16[:], op=ALU.mult,
+            )
+
+        def observe(i, h):
+            vq, vs = st["vq", i]
+            y_ps = psum.tile([P, KP], F32, name="y_ps", tag="y%d" % h, bufs=1)
+            for g in range(GS):
+                nc.tensor.matmul_mx(
+                    out=y_ps[:],
+                    lhsT=vq[:, g * P : (g + 1) * P].bitcast(FP8X4), lhsT_scale=vs[:, g * P : (g + 1) * P],
+                    rhs=hw[:, g, h * 1024 : (h + 1) * 1024].bitcast(FP4X4), rhs_scale=hs[:, g, h * KP : (h + 1) * KP],
+                    start=(g == 0), stop=(g == GS - 1),
+                )
+            st["y", i, h] = y_ps
+
+        def innovation(i, h):
+            if h == 0:
+                st["d", i] = work.tile([P, O], F32, name="d", bufs=2)
+            cols = slice(h * KP, (h + 1) * KP)
+            nc.vector.tensor_tensor(
+                out=st["d", i][:, cols], in0=st["zb", i][:, cols], in1=st["y", i, h][:], op=ALU.subtract
+            )
+
+        def whiten(i):
+            u = work.tile([P, O], F32, name="u", bufs=2)
+            nc.vector.tensor_tensor(out=u[:], in0=st["d", i][:], in1=chan[:, O : 2 * O], op=ALU.mult)
+            st["u", i] = u
+
+        def surprise(i):
+            junk = work.tile([P, O], BF16, name="junk", bufs=1)
+            nc.scalar.activation(out=junk[:], in_=st["u", i][:], func=ACT.Square, accum_out=ssq[:, i, 0:1])
+            nc.gpsimd.tensor_scalar(
+                out=nis_all[:, i : i + 1], in0=ssq[:, i, 0:1], scalar1=1.0 / O, scalar2=0.0, op0=ALU.mult, op1=ALU.add
+            )
+
+        def weight(i):
+            nc.vector.tensor_scalar(
+                out=wden[:, i, 0:1], in0=ssq[:, i, 0:1], scalar1=1.0 / (O * (NU + 1.0)), scalar2=NU / (NU + 1.0),
+                op0=ALU.mult, op1=ALU.add,
+            )
+            nc.vector.reciprocal(out=wgt[:, i, 0:1], in_=wden[:, i, 0:1])
+            if i == NT - 1:
+                nt_ps = psum.tile([P, P], F32, name="nt_ps", tag="xt0", bufs=1)
+                nc.tensor.transpose(nt_ps[:], nis_all[:], ident_f[:])
+                nc.scalar.copy(out=nis_t[:], in_=nt_ps[0:NT, :])
+                nc.scalar.dma_start(out=out_1.rearrange("(i m) o -> i (m o)", m=P), in_=nis_t[:])
+
+        def clip(i):
+            cl = work.tile([P, O], F32, name="cl", bufs=1)
+            nc.vector.tensor_scalar(out=cl[:], in0=st["u", i][:], scalar1=-CLIP, scalar2=CLIP, op0=ALU.max, op1=ALU.min)
+            st["cl", i] = cl
+
+        def times_trust(i):
+            e_sb = work.tile([P, O], BF16, name="e_sb", bufs=2)
+            nc.vector.tensor_tensor(out=e_sb[:], in0=st["cl", i][:], in1=chan[:, 2 * O : 3 * O], op=ALU.mult)
+            st["e", i] = e_sb
+
+        def e_transposes(i):
+            et_ps = psum.tile([P, KP], F32, name="et_ps", tag="et", bufs=1)
+            words = st["e", i][:].bitcast(F32)
+            for k in range(4):
+                h, u = k // 2, k % 2
+                nc.tensor.transpose(et_ps[:, k * P : (k + 1) * P], words[:, 256 * h + u : 256 * (h + 1) : 2], ident_f[:])
+            st["et", i] = et_ps
+
+        def e_copy(i):
+            ei = work.tile([P, O], BF16, name="ei", bufs=2, align_bytes=64)
+            nc.scalar.copy(
+                out=ei[:].bitcast(F32).rearrange("p (h m u) -> p h m u", h=2, u=2),
+                in_=st["et", i][:].rearrange("p (h u m) -> p h m u", h=2, u=2),
+            )
+            st["ei", i] = ei
+
+        def e_quantize(i):
+            eq = work.tile([P, 2 * P], U32, name="eq", bufs=2, align_bytes=64)
+            es = work.tile([P, 2 * P], U8, name="es", bufs=2, align_bytes=64)
+            nc.vector.quantize_mx(out=eq[:].bitcast(FP8X4), scales=es[:], in_=st["ei", i][:])
+            st["eq", i] = (eq, es)
+
+        def update_matmul(i, c):
+            eq, es = st["eq", i]
+            c_ps = psum.tile([P, KP], F32, name="c_ps", tag="acc", bufs=3)
+            for h in range(GO):
+                nc.tensor.matmul_mx(
+                    out=c_ps[:],
+                    lhsT=eq[:, h * P : (h + 1) * P].bitcast(FP8X4), lhsT_scale=es[:, h * P : (h + 1) * P],
+                    rhs=gw[:, h, c * 2048 : (c + 1) * 2048].bitcast(FP8X4), rhs_scale=gs[:, h, c * KP : (c + 1) * KP],
+                    start=(h == 0), stop=(h == GO - 1),
+                )
+            st["c", i, c] = c_ps
+
+        def update_add(i, c):
+            if c == 0:
+                st["out", i] = work.tile([P, S], F32, name="out_sb", bufs=3)
+            out_sb = st["out", i]
+            cols = slice(c * KP, (c + 1) * KP)
+            nc.vector.scalar_tensor_tensor(
+                out=out_sb[:, cols], in0=st["c", i, c][:], scalar=wgt[:, i, 0:1], in1=st["xf", i, c][:],
+                op0=ALU.mult, op1=ALU.add,
+            )
+            if i == NT - 1:
+                nc.sync.dma_start(out=out_0[i * P : (i + 1) * P, cols], in_=out_sb[:, cols])
+            elif c % 2 == 1:
+                half = slice((c - 1) * KP, (c + 1) * KP)
+                nc.sync.dma_start(out=out_0[i * P : (i + 1) * P, half], in_=out_sb[:, half])
+        order = (
+            (3, observe, (0,)),
+            (4, x_affine, (0,)),
+            (1, e_quantize, ()),
+            (2, clip, ()),
+            (1, update_matmul, (0,)),
+            (4, x_affine, (1,)),
+            (0, update_add, (3,)),
+            (2, xf_products, (1,)),
+            (4, z_bias, ()),
+            (3, innovation, (0,)),
+            (1, update_matmul, (1,)),
+            (1, update_add, (0,)),
+            (2, xf_copy, (1,)),
+            (3, observe, (1,)),
+            (2, times_trust, ()),
+            (4, x_copy, (0,)),
+            (2, surprise, ()),
+            (1, update_matmul, (2,)),
+            (1, update_add, (1,)),
+            (2, xf_products, (2,)),
+            (4, x_interleave, ()),
+            (4, x_copy, (1,)),
+            (3, xf_products, (0,)),
+            (2, e_transposes, ()),
+            (2, xf_copy, (2,)),
+            (3, xf_copy, (0,)),
+            (5, x_transposes, (0,)),
+            (3, innovation, (1,)),
+            (5, x_transposes, (1,)),
+            (2, e_copy, ()),
+            (1, update_add, (2,)),
+            (4, x_quantize, ()),
+            (2, xf_products, (3,)),
+            (1, update_matmul, (3,)),
+            (2, weight, ()),
+            (3, whiten, ()),
+            (2, xf_copy, (3,)),
+        )
+        for step in range(-5, NT):
+            for lead, stage, args in order:
+                if 0 <= step + lead < NT and not (stage is z_bias and step + lead < 2):
+                    stage(step + lead, *args)
+                    if stage is x_transposes and step + lead == 0 and args == (1,):
+                        channel_tables()
+                        nc.gpsimd.memset(xts[2][:], 1.0)
+                        nc.gpsimd.memset(nis_all[:], 0.0)
+                        z_bias(0)
+                        z_bias(1)
+                    if stage is x_copy and step + lead == 0 and args == (1,):
+                        for g in range(GS):
+                            build_dmat(g)

@@ -127,18 +127,22 @@ def tile_robust_gain_update_f7_kernel(
                 out=hw_i[:, 2 * k : 2 * k + 2, :], in_=obs_w[2 * k : 2 * k + 2, :, :].rearrange("g p n -> p g n")
             )
         load_z(0)
-        load_x(2)
         load_z(1)
+        load_x(2)
+        load_z(2)
+        load_z(3)
         for q in range(4):
             nc.sync.dma_start(
                 out=gs_i[32 * q : 32 * q + 4, :, :], in_=gain_s[:, 4 * q : 4 * q + 4, :].rearrange("g r n -> r g n")
             )
+        load_x(3)
+        load_z(4)
         for g in range(GO):
             nc.sync.dma_start(out=gw_i[:, g, :], in_=gain_w[g, :, :])
-        for i in range(2, NT):
+        for i in range(5, NT):
+            load_x(i - 1)
             load_z(i)
-            if i + 1 < NT:
-                load_x(i + 1)
+        load_x(NT - 1)
 
         def build_dmat(g):
             for t in range(4):
@@ -192,13 +196,19 @@ def tile_robust_gain_update_f7_kernel(
                         scale=a_sb[:, t, g : g + 1], bias=b_sb[:, t, g : g + 1],
                     )
 
-        def x_interleave(i):
-            vi = work.tile([P, S], BF16, name="vi", bufs=2, align_bytes=64)
-            nc.vector.tensor_copy(
-                out=vi[:].rearrange("p (c i t) -> p c t i", i=4, t=4),
-                in_=st["v", i][:].rearrange("p t (c i) -> p c t i", i=4),
+        def x_group(i, copy, groups):
+            if ("vi", i) not in st:
+                st["vi", i] = work.tile([P, S], BF16, name="vi", bufs=2, align_bytes=64)
+            copy(
+                out=st["vi", i][:].rearrange("p (c i t) -> p c t i", i=4, t=4)[:, groups],
+                in_=st["v", i][:].rearrange("p t (c i) -> p c t i", i=4)[:, groups],
             )
-            st["vi", i] = vi
+
+        def x_group_scalar(i):
+            x_group(i, nc.scalar.copy, slice(0, 48))
+
+        def x_interleave(i):
+            x_group(i, nc.vector.tensor_copy, slice(48, P))
 
         def x_quantize(i):
             vq = work.tile([P, KP], U32, name="vq", bufs=2, align_bytes=64)
@@ -225,10 +235,11 @@ def tile_robust_gain_update_f7_kernel(
             st["xf", i, g] = xf
 
         def z_bias(i):
-            zb = work.tile([P, O], F32, name="zb", bufs=2)
-            for h in range(2):
-                cols = slice(h * O // 2, (h + 1) * O // 2)
-                nc.gpsimd.tensor_tensor(out=zb[:, cols], in0=z_sb[:, i, cols], in1=chan[:, cols], op=ALU.subtract)
+            zb = work.tile([P, O], F32, name="zb", bufs=4)
+            engine, chunks = (nc.gpsimd, 2) if i < 4 else (nc.vector, 1)
+            for h in range(chunks):
+                cols = slice(h * O // chunks, (h + 1) * O // chunks)
+                engine.tensor_tensor(out=zb[:, cols], in0=z_sb[:, i, cols], in1=chan[:, cols], op=ALU.subtract)
             st["zb", i] = zb
             nc.gpsimd.tensor_tensor(
                 out=xfix[:, i, :, :], in0=x_sb[:, i, :].rearrange("p (g r) -> p g r", g=GS)[:, :, KP - 4 : KP],
@@ -338,54 +349,55 @@ def tile_robust_gain_update_f7_kernel(
                 half = slice((c - 1) * KP, (c + 1) * KP)
                 nc.sync.dma_start(out=out_0[i * P : (i + 1) * P, half], in_=out_sb[:, half])
         order = (
-            (3, observe, (0,)),
-            (4, x_affine, (0,)),
-            (1, e_quantize, ()),
-            (2, clip, ()),
-            (1, update_matmul, (0,)),
-            (4, x_affine, (1,)),
+            (2, observe, (0,)),
+            (0, update_add, (0,)),
+            (3, x_affine, (0,)),
+            (1, times_trust, ()),
+            (2, observe, (1,)),
+            (3, x_affine, (1,)),
+            (0, update_add, (1,)),
+            (0, update_matmul, (3,)),
+            (0, update_add, (2,)),
+            (1, e_transposes, ()),
+            (2, innovation, (0,)),
+            (1, xf_products, (1,)),
+            (1, e_copy, ()),
+            (3, z_bias, ()),
+            (1, xf_products, (2,)),
+            (3, x_group_scalar, ()),
+            (4, x_transposes, (0,)),
+            (2, innovation, (1,)),
+            (1, xf_copy, (1,)),
+            (4, x_transposes, (1,)),
             (0, update_add, (3,)),
-            (2, xf_products, (1,)),
-            (4, z_bias, ()),
-            (3, innovation, (0,)),
-            (1, update_matmul, (1,)),
-            (1, update_add, (0,)),
-            (2, xf_copy, (1,)),
-            (3, observe, (1,)),
-            (2, times_trust, ()),
+            (1, xf_copy, (2,)),
+            (3, x_interleave, ()),
+            (1, xf_products, (3,)),
             (4, x_copy, (0,)),
-            (2, surprise, ()),
-            (1, update_matmul, (2,)),
-            (1, update_add, (1,)),
-            (2, xf_products, (2,)),
-            (4, x_interleave, ()),
+            (2, xf_products, (0,)),
+            (1, e_quantize, ()),
+            (1, xf_copy, (3,)),
+            (2, whiten, ()),
+            (1, update_matmul, (0,)),
+            (2, xf_copy, (0,)),
+            (1, update_matmul, (1,)),
             (4, x_copy, (1,)),
-            (3, xf_products, (0,)),
-            (2, e_transposes, ()),
-            (2, xf_copy, (2,)),
-            (3, xf_copy, (0,)),
-            (5, x_transposes, (0,)),
-            (3, innovation, (1,)),
-            (5, x_transposes, (1,)),
-            (2, e_copy, ()),
-            (1, update_add, (2,)),
-            (4, x_quantize, ()),
-            (2, xf_products, (3,)),
-            (1, update_matmul, (3,)),
-            (2, weight, ()),
-            (3, whiten, ()),
-            (2, xf_copy, (3,)),
+            (1, weight, ()),
+            (3, x_quantize, ()),
+            (1, update_matmul, (2,)),
+            (2, surprise, ()),
+            (2, clip, ()),
         )
-        for step in range(-5, NT):
+        for step in range(-4, NT):
             for lead, stage, args in order:
-                if 0 <= step + lead < NT and not (stage is z_bias and step + lead < 2):
+                if 0 <= step + lead < NT and not (stage is z_bias and step + lead < 4):
                     stage(step + lead, *args)
                     if stage is x_transposes and step + lead == 0 and args == (1,):
                         channel_tables()
                         nc.gpsimd.memset(xts[2][:], 1.0)
                         nc.gpsimd.memset(nis_all[:], 0.0)
-                        z_bias(0)
-                        z_bias(1)
-                    if stage is x_copy and step + lead == 0 and args == (1,):
+                        for i in range(4):
+                            z_bias(i)
+                    if stage is x_group_scalar and step + lead == 0:
                         for g in range(GS):
                             build_dmat(g)

@@ -33,7 +33,6 @@ def tile_robust_gain_update_f7_kernel(
         keep = ctx.enter_context(tc.tile_pool(name="keep", bufs=1))
         work = ctx.enter_context(tc.tile_pool(name="work", bufs=2))
         psum = ctx.enter_context(tc.psum_pool(name="psum", bufs=1))
-        ctx.enter_context(tc.manual_schedule())
 
         ident_f = keep.tile([P, P], F32, name="ident_f")
         ident_b = keep.tile([P, P], BF16, name="ident_b")
@@ -57,10 +56,9 @@ def tile_robust_gain_update_f7_kernel(
         chan = keep.tile([P, 3 * O], BF16, name="chan")
         dec16 = keep.tile([P, GS, 4], BF16, name="dec16")
         xfix = keep.tile([P, NT, GS, 4], F32, name="xfix")
-        ssq = keep.tile([P, NT, 8], F32, name="ssq")
+        ssq = keep.tile([P, P], F32, name="ssq")
         wden = keep.tile([P, NT, 8], F32, name="wden")
         wgt = keep.tile([P, NT, 8], F32, name="wgt")
-        nis_all = keep.tile([P, P], F32, name="nis_all")
         nis_t = keep.tile([NT, P], F32, name="nis_t")
 
 
@@ -205,10 +203,10 @@ def tile_robust_gain_update_f7_kernel(
             )
 
         def x_group_scalar(i):
-            x_group(i, nc.scalar.copy, slice(0, 48))
+            x_group(i, nc.scalar.copy, slice(0, 64))
 
         def x_interleave(i):
-            x_group(i, nc.vector.tensor_copy, slice(48, P))
+            x_group(i, nc.vector.tensor_copy, slice(64, P))
 
         def x_quantize(i):
             vq = work.tile([P, KP], U32, name="vq", bufs=2, align_bytes=64)
@@ -231,7 +229,6 @@ def tile_robust_gain_update_f7_kernel(
             nc.scalar.copy(
                 out=xf[:].rearrange("p (j t) -> p j t", t=4), in_=st["xf_ps", i, g][:].rearrange("p (t j) -> p j t", t=4)
             )
-            nc.gpsimd.tensor_tensor(out=xf[:, KP - 4 : KP], in0=xf[:, KP - 4 : KP], in1=xfix[:, i, g, :], op=ALU.add)
             st["xf", i, g] = xf
 
         def z_bias(i):
@@ -273,21 +270,18 @@ def tile_robust_gain_update_f7_kernel(
 
         def surprise(i):
             junk = work.tile([P, O], BF16, name="junk", bufs=1)
-            nc.scalar.activation(out=junk[:], in_=st["u", i][:], func=ACT.Square, accum_out=ssq[:, i, 0:1])
+            nc.scalar.activation(out=junk[:], in_=st["u", i][:], func=ACT.Square, accum_out=ssq[:, i : i + 1])
             nc.gpsimd.tensor_scalar(
-                out=nis_all[:, i : i + 1], in0=ssq[:, i, 0:1], scalar1=1.0 / O, scalar2=0.0, op0=ALU.mult, op1=ALU.add
+                out=wden[:, i, 0:1], in0=ssq[:, i : i + 1], scalar1=1.0 / (O * (NU + 1.0)), scalar2=NU / (NU + 1.0),
+                op0=ALU.mult, op1=ALU.add,
             )
 
         def weight(i):
-            nc.vector.tensor_scalar(
-                out=wden[:, i, 0:1], in0=ssq[:, i, 0:1], scalar1=1.0 / (O * (NU + 1.0)), scalar2=NU / (NU + 1.0),
-                op0=ALU.mult, op1=ALU.add,
-            )
             nc.vector.reciprocal(out=wgt[:, i, 0:1], in_=wden[:, i, 0:1])
             if i == NT - 1:
                 nt_ps = psum.tile([P, P], F32, name="nt_ps", tag="xt0", bufs=1)
-                nc.tensor.transpose(nt_ps[:], nis_all[:], ident_f[:])
-                nc.scalar.copy(out=nis_t[:], in_=nt_ps[0:NT, :])
+                nc.tensor.transpose(nt_ps[:], ssq[:], ident_f[:])
+                nc.scalar.activation(out=nis_t[:], in_=nt_ps[0:NT, :], func=ACT.Copy, scale=1.0 / O)
                 nc.scalar.dma_start(out=out_1.rearrange("(i m) o -> i (m o)", m=P), in_=nis_t[:])
 
         def clip(i):
@@ -344,9 +338,13 @@ def tile_robust_gain_update_f7_kernel(
                 op0=ALU.mult, op1=ALU.add,
             )
             if i == NT - 1:
+                last = out_sb[:, (c + 1) * KP - 4 : (c + 1) * KP]
+                nc.gpsimd.tensor_tensor(out=last, in0=last, in1=xfix[:, i, c, :], op=ALU.add)
                 nc.sync.dma_start(out=out_0[i * P : (i + 1) * P, cols], in_=out_sb[:, cols])
             elif c % 2 == 1:
                 half = slice((c - 1) * KP, (c + 1) * KP)
+                last = out_sb[:, half].rearrange("p (g r) -> p g r", g=2)[:, :, KP - 4 : KP]
+                nc.gpsimd.tensor_tensor(out=last, in0=last, in1=xfix[:, i, c - 1 : c + 1, :], op=ALU.add)
                 nc.sync.dma_start(out=out_0[i * P : (i + 1) * P, half], in_=out_sb[:, half])
         order = (
             (2, observe, (0,)),
@@ -395,7 +393,7 @@ def tile_robust_gain_update_f7_kernel(
                     if stage is x_transposes and step + lead == 0 and args == (1,):
                         channel_tables()
                         nc.gpsimd.memset(xts[2][:], 1.0)
-                        nc.gpsimd.memset(nis_all[:], 0.0)
+                        nc.gpsimd.memset(ssq[:], 0.0)
                         for i in range(4):
                             z_bias(i)
                     if stage is x_group_scalar and step + lead == 0:

@@ -33,6 +33,7 @@ def tile_robust_gain_update_f7_kernel(
         keep = ctx.enter_context(tc.tile_pool(name="keep", bufs=1))
         work = ctx.enter_context(tc.tile_pool(name="work", bufs=2))
         psum = ctx.enter_context(tc.psum_pool(name="psum", bufs=1))
+        ctx.enter_context(tc.manual_schedule())
 
         ident_f = keep.tile([P, P], F32, name="ident_f")
         ident_b = keep.tile([P, P], BF16, name="ident_b")
@@ -69,18 +70,23 @@ def tile_robust_gain_update_f7_kernel(
             nc.scalar.dma_start(out=vec_rows[4 * i : 4 * i + 4, :], in_=v.rearrange("(g r) -> g r", r=KP))
         for hh in range(2):
             nc.sync.dma_start(out=x_sb[:, 0, hh * 1024 : (hh + 1) * 1024], in_=x[0:P, hh * 1024 : (hh + 1) * 1024])
-        nc.vector.memset(hs[:].rearrange("p g n -> p (g n)").bitcast(I32), 0)
-        nc.vector.memset(ones_b[:], 1.0)
+        nc.scalar.copy(
+            out=ident_rep[:].rearrange("p (g j t) -> p g j t", g=GS, t=4),
+            in_=ident_b[:].unsqueeze(1).unsqueeze(3).to_broadcast([P, GS, P, 4]),
+        )
+        nc.scalar.dma_start(out=ident_rep[P - 1 : P, :], in_=drift.rearrange("(o n) -> o n", o=1))
         nc.vector.memset(chan_rows[:], 0.0)
-        nc.vector.memset(xts[0][:], 1.0)
-        nc.gpsimd.memset(xts[1][:], 1.0)
         for i, v in enumerate((obs_bias, rinv, trust)):
             nc.gpsimd.dma_start(out=chan_rows[0:1, i * O : (i + 1) * O], in_=v.rearrange("(o n) -> o n", o=1))
-        nc.gpsimd.dma_start(
+        nc.vector.memset(hs[:].rearrange("p g n -> p (g n)").bitcast(I32), 0)
+        nc.vector.memset(ones_b[:], 1.0)
+        nc.vector.memset(xts[0][:], 1.0)
+        nc.gpsimd.memset(gs[:].rearrange("p g n -> p (g n)").bitcast(I32), 0)
+        nc.gpsimd.memset(xts[1][:], 1.0)
+        nc.scalar.dma_start(
             out=chan_rows[0:1, 3 * O : 3 * O + 16].rearrange("o (g r) -> o g r", r=4),
             in_=decay.rearrange("(o g r) -> o g r", o=1, r=KP)[:, :, KP - 4 : KP],
         )
-        nc.gpsimd.memset(gs[:].rearrange("p g n -> p (g n)").bitcast(I32), 0)
 
         hs_i = hs[:].rearrange("p g n -> p (g n)").bitcast(I32).rearrange("p (g n) -> p g n", g=GS)
         hw_i = hw[:].rearrange("p g n -> p (g n)").bitcast(I32).rearrange("p (g n) -> p g n", g=GS)
@@ -103,11 +109,6 @@ def tile_robust_gain_update_f7_kernel(
         nc.vector.tensor_copy(out=pv[:], in_=pv_ps[:, :, 0:12])
         nc.vector.tensor_tensor(out=a_sb[:], in0=pv[:, :, 0:4], in1=pv[:, :, 8:12], op=ALU.mult)
         nc.vector.tensor_tensor(out=b_sb[:], in0=pv[:, :, 4:8], in1=pv[:, :, 8:12], op=ALU.mult)
-        nc.vector.tensor_copy(
-            out=ident_rep[:].rearrange("p (g j t) -> p g j t", g=GS, t=4),
-            in_=ident_b[:].unsqueeze(1).unsqueeze(3).to_broadcast([P, GS, P, 4]),
-        )
-        nc.gpsimd.dma_start(out=ident_rep[P - 1 : P, :], in_=drift.rearrange("(o n) -> o n", o=1))
         nc.gpsimd.tensor_scalar(
             out=kcol[:], in0=ident_f[:, P - 1 : P], scalar1=-1.0, scalar2=1.0, op0=ALU.mult, op1=ALU.add
         )
@@ -124,8 +125,7 @@ def tile_robust_gain_update_f7_kernel(
             nc.sync.dma_start(
                 out=hw_i[:, 2 * k : 2 * k + 2, :], in_=obs_w[2 * k : 2 * k + 2, :, :].rearrange("g p n -> p g n")
             )
-        load_z(0)
-        load_z(1)
+            load_z(k)
         load_x(2)
         load_z(2)
         load_z(3)
@@ -144,12 +144,12 @@ def tile_robust_gain_update_f7_kernel(
 
         def build_dmat(g):
             for t in range(4):
-                nc.scalar.activation(
-                    out=dmat[:, g, t, :], in_=ident_rep[:].rearrange("p (g j t) -> p g j t", g=GS, t=4)[:, g, :, t],
-                    func=ACT.Copy, scale=decm[:, t, g : g + 1],
+                nc.gpsimd.tensor_scalar(
+                    out=dmat[:, g, t, :], in0=ident_rep[:].rearrange("p (g j t) -> p g j t", g=GS, t=4)[:, g, :, t],
+                    scalar1=decm[:, t, g : g + 1], scalar2=0.0, op0=ALU.mult, op1=ALU.add,
                 )
 
-        def channel_tables():
+        def channel_matmuls():
             for k in range(3):
                 cb_ps = psum.tile([P, O], BF16, name="cb_ps", tag="acc", bufs=3)
                 for h in range(2):
@@ -157,10 +157,13 @@ def tile_robust_gain_update_f7_kernel(
                     nc.tensor.matmul(
                         cb_ps[:, h * KP : (h + 1) * KP], lhsT=ones_b[:], rhs=chan_rows[:, cols], start=True, stop=True
                     )
-                nc.vector.tensor_copy(out=chan[:, k * O : (k + 1) * O], in_=cb_ps[:])
-            d16_ps = psum.tile([P, 16], F32, name="d16_ps", tag="acc", bufs=3)
+                st["cb", k] = cb_ps
+            d16_ps = psum.tile([P, 16], F32, name="d16_ps", tag="et", bufs=1)
             nc.tensor.matmul(d16_ps[:], lhsT=ones_b[:], rhs=chan_rows[:, 3 * O : 3 * O + 16], start=True, stop=True)
-            nc.vector.tensor_copy(out=dec16[:].rearrange("p g r -> p (g r)"), in_=d16_ps[:])
+            st["d16"] = d16_ps
+
+        def channel_copy(k, copy):
+            copy(out=chan[:, k * O : (k + 1) * O], in_=st["cb", k][:])
 
         st = {}
 
@@ -189,6 +192,12 @@ def tile_robust_gain_update_f7_kernel(
                 g, u = 2 * hh + k // 2, k % 2
                 for e in range(2):
                     t = 2 * u + e
+                    if i == 0 and hh == 1:
+                        nc.vector.tensor_scalar(
+                            out=v[:, t, g * P : (g + 1) * P], in0=pairs[:, k, :, e], scalar1=a_sb[:, t, g : g + 1],
+                            scalar2=b_sb[:, t, g : g + 1], op0=ALU.mult, op1=ALU.add,
+                        )
+                        continue
                     nc.scalar.activation(
                         out=v[:, t, g * P : (g + 1) * P], in_=pairs[:, k, :, e], func=ACT.Identity,
                         scale=a_sb[:, t, g : g + 1], bias=b_sb[:, t, g : g + 1],
@@ -203,10 +212,10 @@ def tile_robust_gain_update_f7_kernel(
             )
 
         def x_group_scalar(i):
-            x_group(i, nc.scalar.copy, slice(0, 64))
+            x_group(i, nc.scalar.copy, slice(0, 24))
 
         def x_interleave(i):
-            x_group(i, nc.vector.tensor_copy, slice(64, P))
+            x_group(i, nc.vector.tensor_copy, slice(24, P))
 
         def x_quantize(i):
             vq = work.tile([P, KP], U32, name="vq", bufs=2, align_bytes=64)
@@ -231,13 +240,13 @@ def tile_robust_gain_update_f7_kernel(
             )
             st["xf", i, g] = xf
 
-        def z_bias(i):
-            zb = work.tile([P, O], F32, name="zb", bufs=4)
-            engine, chunks = (nc.gpsimd, 2) if i < 4 else (nc.vector, 1)
-            for h in range(chunks):
-                cols = slice(h * O // chunks, (h + 1) * O // chunks)
-                engine.tensor_tensor(out=zb[:, cols], in0=z_sb[:, i, cols], in1=chan[:, cols], op=ALU.subtract)
-            st["zb", i] = zb
+        def z_bias(i, h):
+            zb = work.tile([P, KP], F32, name="zb", tag="zb%d" % h, bufs=1)
+            cols = slice(h * KP, (h + 1) * KP)
+            nc.gpsimd.tensor_tensor(out=zb[:], in0=z_sb[:, i, cols], in1=chan[:, cols], op=ALU.subtract)
+            st["zb", i, h] = zb
+
+        def fix_columns(i):
             nc.gpsimd.tensor_tensor(
                 out=xfix[:, i, :, :], in0=x_sb[:, i, :].rearrange("p (g r) -> p g r", g=GS)[:, :, KP - 4 : KP],
                 in1=dec16[:], op=ALU.mult,
@@ -260,7 +269,7 @@ def tile_robust_gain_update_f7_kernel(
                 st["d", i] = work.tile([P, O], F32, name="d", bufs=2)
             cols = slice(h * KP, (h + 1) * KP)
             nc.vector.tensor_tensor(
-                out=st["d", i][:, cols], in0=st["zb", i][:, cols], in1=st["y", i, h][:], op=ALU.subtract
+                out=st["d", i][:, cols], in0=st["zb", i, h][:], in1=st["y", i, h][:], op=ALU.subtract
             )
 
         def whiten(i):
@@ -271,15 +280,16 @@ def tile_robust_gain_update_f7_kernel(
         def surprise(i):
             junk = work.tile([P, O], BF16, name="junk", bufs=1)
             nc.scalar.activation(out=junk[:], in_=st["u", i][:], func=ACT.Square, accum_out=ssq[:, i : i + 1])
-            nc.gpsimd.tensor_scalar(
-                out=wden[:, i, 0:1], in0=ssq[:, i : i + 1], scalar1=1.0 / (O * (NU + 1.0)), scalar2=NU / (NU + 1.0),
-                op0=ALU.mult, op1=ALU.add,
+
+        def weight_denominator(i):
+            nc.scalar.activation(
+                out=wden[:, i, 0:1], in_=ssq[:, i : i + 1], func=ACT.Copy, scale=1.0 / (O * (NU + 1.0)), bias=NU / (NU + 1.0)
             )
 
         def weight(i):
             nc.vector.reciprocal(out=wgt[:, i, 0:1], in_=wden[:, i, 0:1])
             if i == NT - 1:
-                nt_ps = psum.tile([P, P], F32, name="nt_ps", tag="xt0", bufs=1)
+                nt_ps = psum.tile([P, P], F32, name="nt_ps", tag="y0", bufs=1)
                 nc.tensor.transpose(nt_ps[:], ssq[:], ident_f[:])
                 nc.scalar.activation(out=nis_t[:], in_=nt_ps[0:NT, :], func=ACT.Copy, scale=1.0 / O)
                 nc.scalar.dma_start(out=out_1.rearrange("(i m) o -> i (m o)", m=P), in_=nis_t[:])
@@ -348,54 +358,68 @@ def tile_robust_gain_update_f7_kernel(
                 nc.sync.dma_start(out=out_0[i * P : (i + 1) * P, half], in_=out_sb[:, half])
         order = (
             (2, observe, (0,)),
-            (0, update_add, (0,)),
-            (3, x_affine, (0,)),
-            (1, times_trust, ()),
-            (2, observe, (1,)),
-            (3, x_affine, (1,)),
             (0, update_add, (1,)),
+            (3, x_affine, (1,)),
+            (2, observe, (1,)),
+            (1, times_trust, ()),
+            (1, surprise, ()),
             (0, update_matmul, (3,)),
-            (0, update_add, (2,)),
-            (1, e_transposes, ()),
             (2, innovation, (0,)),
             (1, xf_products, (1,)),
-            (1, e_copy, ()),
-            (3, z_bias, ()),
-            (1, xf_products, (2,)),
-            (3, x_group_scalar, ()),
-            (4, x_transposes, (0,)),
-            (2, innovation, (1,)),
-            (1, xf_copy, (1,)),
-            (4, x_transposes, (1,)),
-            (0, update_add, (3,)),
-            (1, xf_copy, (2,)),
             (3, x_interleave, ()),
-            (1, xf_products, (3,)),
-            (4, x_copy, (0,)),
-            (2, xf_products, (0,)),
-            (1, e_quantize, ()),
-            (1, xf_copy, (3,)),
-            (2, whiten, ()),
-            (1, update_matmul, (0,)),
-            (2, xf_copy, (0,)),
-            (1, update_matmul, (1,)),
-            (4, x_copy, (1,)),
+            (1, e_transposes, ()),
+            (3, x_copy, (1,)),
+            (1, weight_denominator, ()),
+            (4, x_transposes, (0,)),
+            (3, x_group_scalar, ()),
+            (3, z_bias, (0,)),
+            (3, fix_columns, ()),
+            (0, update_add, (2,)),
+            (1, e_copy, ()),
             (1, weight, ()),
+            (0, update_add, (3,)),
+            (2, xf_products, (0,)),
+            (1, xf_copy, (1,)),
+            (2, innovation, (1,)),
+            (1, xf_products, (2,)),
+            (2, xf_copy, (0,)),
+            (1, xf_products, (3,)),
+            (1, e_quantize, ()),
+            (1, xf_copy, (2,)),
+            (2, whiten, ()),
+            (4, x_transposes, (1,)),
+            (4, x_copy, (0,)),
+            (1, update_matmul, (0,)),
+            (1, xf_copy, (3,)),
             (3, x_quantize, ()),
-            (1, update_matmul, (2,)),
-            (2, surprise, ()),
+            (1, update_matmul, (1,)),
+            (4, x_affine, (0,)),
             (2, clip, ()),
+            (1, update_matmul, (2,)),
+            (3, z_bias, (1,)),
+            (1, update_add, (0,)),
         )
+        x_transposes(0, 0)
+        x_transposes(0, 1)
+        channel_matmuls()
+        x_affine(0, 0)
+        x_affine(0, 1)
+        x_copy(0, 0)
+        x_copy(0, 1)
+        x_group_scalar(0)
+        x_interleave(0)
+        channel_copy(0, nc.scalar.copy)
+        nc.scalar.copy(out=dec16[:].rearrange("p g r -> p (g r)"), in_=st["d16"][:])
+        x_quantize(0)
+        channel_copy(1, nc.vector.tensor_copy)
+        channel_copy(2, nc.vector.tensor_copy)
+        for g in range(GS):
+            build_dmat(g)
+        done = (x_transposes, x_affine, x_copy, x_group_scalar, x_interleave, x_quantize)
         for step in range(-4, NT):
             for lead, stage, args in order:
-                if 0 <= step + lead < NT and not (stage is z_bias and step + lead < 4):
+                if 0 <= step + lead < NT and not (step + lead == 0 and stage in done):
                     stage(step + lead, *args)
-                    if stage is x_transposes and step + lead == 0 and args == (1,):
-                        channel_tables()
-                        nc.gpsimd.memset(xts[2][:], 1.0)
-                        nc.gpsimd.memset(ssq[:], 0.0)
-                        for i in range(4):
-                            z_bias(i)
-                    if stage is x_group_scalar and step + lead == 0:
-                        for g in range(GS):
-                            build_dmat(g)
+                if step + lead == 0 and stage is z_bias and args == (1,):
+                    nc.gpsimd.memset(xts[2][:], 1.0)
+                    nc.gpsimd.memset(ssq[:], 0.0)

from contextlib import ExitStack

import concourse.mybir as mybir
from concourse.masks import make_identity

M, S, O = 1024, 2048, 1024
NU = 4.0
CLIP = 2.5
FLOPS = 2 * 2 * M * S * O

F32 = mybir.dt.float32
BF16 = mybir.dt.bfloat16
I32 = mybir.dt.int32
U32 = mybir.dt.uint32
U8 = mybir.dt.uint8
FP8X4 = mybir.dt.float8_e4m3fn_x4
FP4X4 = mybir.dt.float4_e2m1fn_x4
ACT = mybir.ActivationFunctionType
ALU = mybir.AluOpType

P = 128
KP = 512
NT = M // P
GS = S // KP
GO = O // KP


def tile_robust_gain_update_f7_kernel(
    tc, x, z, decay, drift, unit, obs_words, obs_scales, obs_bias, rinv, trust, gain_words, gain_scales, out_0, out_1
):
    nc = tc.nc
    with ExitStack() as ctx:
        keep = ctx.enter_context(tc.tile_pool(name="keep", bufs=1))
        work = ctx.enter_context(tc.tile_pool(name="work", bufs=2))
        psum = ctx.enter_context(tc.psum_pool(name="psum", bufs=1))
        ctx.enter_context(tc.manual_schedule())

        ident_f = keep.tile([P, P], F32, name="ident_f")
        ident_b = keep.tile([P, P], BF16, name="ident_b")
        ones_b = keep.tile([P, P], BF16, name="ones_b")
        vec_rows = keep.tile([P, KP], BF16, name="vec_rows")
        chan_rows = keep.tile([P, 3 * O + 16], BF16, name="chan_rows")
        ident_rep = keep.tile([P, S], BF16, name="ident_rep")
        hw = keep.tile([P, GS, 2 * O], U8, name="hw", align_bytes=64)
        hs = keep.tile([P, GS, O], U8, name="hs", align_bytes=64)
        gw = keep.tile([P, GO, 4 * S], U8, name="gw", align_bytes=64)
        gs = keep.tile([P, GO, S], U8, name="gs", align_bytes=64)
        x_sb = keep.tile([P, NT, S], BF16, name="x_sb")
        z_sb = keep.tile([P, NT, O], BF16, name="z_sb")
        xts = [keep.tile([P, S], BF16, name="xts%d" % i) for i in range(3)]
        pv = keep.tile([P, 4, 12], F32, name="pv")
        a_sb = keep.tile([P, 4, GS], F32, name="a_sb")
        b_sb = keep.tile([P, 4, GS], F32, name="b_sb")
        kcol = keep.tile([P, 1], F32, name="kcol")
        decm = keep.tile([P, 4, GS], F32, name="decm")
        dmat = keep.tile([P, GS, 4, P], BF16, name="dmat")
        chan = keep.tile([P, 3 * O], BF16, name="chan")
        dec16 = keep.tile([P, GS, 4], BF16, name="dec16")
        xfix = keep.tile([P, NT, GS, 4], F32, name="xfix")
        ssq = keep.tile([P, P], F32, name="ssq")
        wden = keep.tile([P, NT, 8], F32, name="wden")
        wgt = keep.tile([P, NT, 8], F32, name="wgt")
        nis_t = keep.tile([NT, P], F32, name="nis_t")


        make_identity(nc, ident_b[:])
        make_identity(nc, ident_f[:])
        nc.vector.memset(vec_rows[:], 0.0)
        for i, v in enumerate((decay, drift, unit)):
            nc.scalar.dma_start(out=vec_rows[4 * i : 4 * i + 4, :], in_=v.rearrange("(g r) -> g r", r=KP))
        for hh in range(2):
            nc.sync.dma_start(out=x_sb[:, 0, hh * 1024 : (hh + 1) * 1024], in_=x[0:P, hh * 1024 : (hh + 1) * 1024])
        nc.scalar.copy(
            out=ident_rep[:].rearrange("p (g j t) -> p g j t", g=GS, t=4),
            in_=ident_b[:].unsqueeze(1).unsqueeze(3).to_broadcast([P, GS, P, 4]),
        )
        nc.scalar.dma_start(out=ident_rep[P - 1 : P, :], in_=drift.rearrange("(o n) -> o n", o=1))
        nc.vector.memset(chan_rows[:], 0.0)
        for i, v in enumerate((obs_bias, rinv, trust)):
            nc.gpsimd.dma_start(out=chan_rows[0:1, i * O : (i + 1) * O], in_=v.rearrange("(o n) -> o n", o=1))
        nc.vector.memset(hs[:].rearrange("p g n -> p (g n)").bitcast(I32), 0)
        nc.vector.memset(ones_b[:], 1.0)
        nc.vector.memset(xts[0][:], 1.0)
        nc.gpsimd.memset(gs[:].rearrange("p g n -> p (g n)").bitcast(I32), 0)
        nc.gpsimd.memset(xts[1][:], 1.0)
        nc.scalar.dma_start(
            out=chan_rows[0:1, 3 * O : 3 * O + 16].rearrange("o (g r) -> o g r", r=4),
            in_=decay.rearrange("(o g r) -> o g r", o=1, r=KP)[:, :, KP - 4 : KP],
        )

        hs_i = hs[:].rearrange("p g n -> p (g n)").bitcast(I32).rearrange("p (g n) -> p g n", g=GS)
        hw_i = hw[:].rearrange("p g n -> p (g n)").bitcast(I32).rearrange("p (g n) -> p g n", g=GS)
        gs_i = gs[:].rearrange("p g n -> p (g n)").bitcast(I32).rearrange("p (g n) -> p g n", g=GO)
        gw_i = gw[:].rearrange("p g n -> p (g n)").bitcast(I32).rearrange("p (g n) -> p g n", g=GO)
        obs_w = obs_words.bitcast(I32)
        obs_s = obs_scales.bitcast(I32)
        gain_w = gain_words.rearrange("g p n t -> g p (n t)").bitcast(I32)
        gain_s = gain_scales.bitcast(I32)

        def load_x(i):
            nc.sync.dma_start(out=x_sb[:, i, :], in_=x[i * P : (i + 1) * P, :])

        def load_z(i):
            nc.sync.dma_start(out=z_sb[:, i, :], in_=z[i * P : (i + 1) * P, :])

        pv_ps = psum.tile([P, 4, P], BF16, name="pv_ps", tag="et", bufs=1)
        for t in range(4):
            nc.tensor.transpose(pv_ps[:, t, :], vec_rows[:, t : KP : 4], ident_b[:])
        nc.vector.tensor_copy(out=pv[:], in_=pv_ps[:, :, 0:12])
        nc.vector.tensor_tensor(out=a_sb[:], in0=pv[:, :, 0:4], in1=pv[:, :, 8:12], op=ALU.mult)
        nc.vector.tensor_tensor(out=b_sb[:], in0=pv[:, :, 4:8], in1=pv[:, :, 8:12], op=ALU.mult)
        nc.gpsimd.tensor_scalar(
            out=kcol[:], in0=ident_f[:, P - 1 : P], scalar1=-1.0, scalar2=1.0, op0=ALU.mult, op1=ALU.add
        )
        nc.gpsimd.tensor_scalar(
            out=decm[:], in0=pv[:, :, 0:4], scalar1=kcol[:, 0:1], scalar2=ident_f[:, P - 1 : P], op0=ALU.mult, op1=ALU.add
        )

        for q in range(4):
            nc.sync.dma_start(
                out=hs_i[32 * q : 32 * q + 4, :, :], in_=obs_s[:, 4 * q : 4 * q + 4, :].rearrange("g r n -> r g n")
            )
        load_x(1)
        for k in range(2):
            nc.sync.dma_start(
                out=hw_i[:, 2 * k : 2 * k + 2, :], in_=obs_w[2 * k : 2 * k + 2, :, :].rearrange("g p n -> p g n")
            )
            load_z(k)
        load_x(2)
        load_z(2)
        load_z(3)
        for q in range(4):
            nc.sync.dma_start(
                out=gs_i[32 * q : 32 * q + 4, :, :], in_=gain_s[:, 4 * q : 4 * q + 4, :].rearrange("g r n -> r g n")
            )
        load_x(3)
        load_z(4)
        for g in range(GO):
            nc.sync.dma_start(out=gw_i[:, g, :], in_=gain_w[g, :, :])
        for i in range(5, NT):
            load_x(i - 1)
            load_z(i)
        load_x(NT - 1)

        def build_dmat(g):
            for t in range(4):
                nc.gpsimd.tensor_scalar(
                    out=dmat[:, g, t, :], in0=ident_rep[:].rearrange("p (g j t) -> p g j t", g=GS, t=4)[:, g, :, t],
                    scalar1=decm[:, t, g : g + 1], scalar2=0.0, op0=ALU.mult, op1=ALU.add,
                )

        def channel_matmuls():
            for k in range(3):
                cb_ps = psum.tile([P, O], BF16, name="cb_ps", tag="acc", bufs=3)
                for h in range(2):
                    cols = slice(k * O + h * KP, k * O + (h + 1) * KP)
                    nc.tensor.matmul(
                        cb_ps[:, h * KP : (h + 1) * KP], lhsT=ones_b[:], rhs=chan_rows[:, cols], start=True, stop=True
                    )
                st["cb", k] = cb_ps
            d16_ps = psum.tile([P, 16], F32, name="d16_ps", tag="et", bufs=1)
            nc.tensor.matmul(d16_ps[:], lhsT=ones_b[:], rhs=chan_rows[:, 3 * O : 3 * O + 16], start=True, stop=True)
            st["d16"] = d16_ps

        def channel_copy(k, copy):
            copy(out=chan[:, k * O : (k + 1) * O], in_=st["cb", k][:])

        st = {}

        def x_transposes(i, hh):
            xt_ps = psum.tile([P, KP], F32, name="xt_ps", tag="xt%d" % hh, bufs=1)
            words = x_sb[:, i, :].bitcast(F32)
            for k in range(4):
                g, u = 2 * hh + k // 2, k % 2
                nc.tensor.transpose(
                    xt_ps[:, k * P : (k + 1) * P], words[:, 256 * g + u : 256 * (g + 1) : 2], ident_f[:]
                )
            st["xt", i, hh] = xt_ps

        def x_copy(i, hh):
            nc.scalar.copy(
                out=xts[i % 3][0 : P - 1, hh * 1024 : (hh + 1) * 1024].bitcast(F32),
                in_=st["xt", i, hh][0 : P - 1, :],
            )

        def x_affine(i, hh):
            if hh == 0:
                st["v", i] = work.tile([P, 4, KP], BF16, name="v", bufs=2)
            v = st["v", i]
            pairs = st["xt", i, hh][:].bitcast(BF16).rearrange("p (k m e) -> p k m e", k=4, e=2)
            for k in range(4):
                g, u = 2 * hh + k // 2, k % 2
                for e in range(2):
                    t = 2 * u + e
                    if i == 0 and hh == 1:
                        nc.vector.tensor_scalar(
                            out=v[:, t, g * P : (g + 1) * P], in0=pairs[:, k, :, e], scalar1=a_sb[:, t, g : g + 1],
                            scalar2=b_sb[:, t, g : g + 1], op0=ALU.mult, op1=ALU.add,
                        )
                        continue
                    nc.scalar.activation(
                        out=v[:, t, g * P : (g + 1) * P], in_=pairs[:, k, :, e], func=ACT.Identity,
                        scale=a_sb[:, t, g : g + 1], bias=b_sb[:, t, g : g + 1],
                    )

        def x_group(i, copy, groups):
            if ("vi", i) not in st:
                st["vi", i] = work.tile([P, S], BF16, name="vi", bufs=2, align_bytes=64)
            copy(
                out=st["vi", i][:].rearrange("p (c i t) -> p c t i", i=4, t=4)[:, groups],
                in_=st["v", i][:].rearrange("p t (c i) -> p c t i", i=4)[:, groups],
            )

        def x_group_scalar(i):
            x_group(i, nc.scalar.copy, slice(0, 24))

        def x_interleave(i):
            x_group(i, nc.vector.tensor_copy, slice(24, P))

        def x_quantize(i):
            vq = work.tile([P, KP], U32, name="vq", bufs=2, align_bytes=64)
            vs = work.tile([P, KP], U8, name="vs", bufs=2, align_bytes=64)
            nc.vector.quantize_mx(out=vq[:].bitcast(FP8X4), scales=vs[:], in_=st["vi", i][:])
            st["vq", i] = (vq, vs)

        def xf_products(i, g):
            rows = xts[i % 3][:].rearrange("p (k m e) -> p k m e", k=8, e=2)
            xf_ps = psum.tile([P, KP], F32, name="xf_ps", tag="acc", bufs=3)
            for t in range(4):
                nc.tensor.matmul(
                    xf_ps[:, t * P : (t + 1) * P], lhsT=rows[:, 2 * g + t // 2, :, t % 2], rhs=dmat[:, g, t, :],
                    start=True, stop=True,
                )
            st["xf_ps", i, g] = xf_ps

        def xf_copy(i, g):
            xf = work.tile([P, KP], F32, name="xf", tag="xf%d" % g, bufs=2)
            nc.scalar.copy(
                out=xf[:].rearrange("p (j t) -> p j t", t=4), in_=st["xf_ps", i, g][:].rearrange("p (t j) -> p j t", t=4)
            )
            st["xf", i, g] = xf

        def z_bias(i, h):
            zb = work.tile([P, KP], F32, name="zb", tag="zb%d" % h, bufs=1)
            cols = slice(h * KP, (h + 1) * KP)
            nc.gpsimd.tensor_tensor(out=zb[:], in0=z_sb[:, i, cols], in1=chan[:, cols], op=ALU.subtract)
            st["zb", i, h] = zb

        def fix_columns(i):
            nc.gpsimd.tensor_tensor(
                out=xfix[:, i, :, :], in0=x_sb[:, i, :].rearrange("p (g r) -> p g r", g=GS)[:, :, KP - 4 : KP],
                in1=dec16[:], op=ALU.mult,
            )

        def observe(i, h):
            vq, vs = st["vq", i]
            y_ps = psum.tile([P, KP], F32, name="y_ps", tag="y%d" % h, bufs=1)
            for g in range(GS):
                nc.tensor.matmul_mx(
                    out=y_ps[:],
                    lhsT=vq[:, g * P : (g + 1) * P].bitcast(FP8X4), lhsT_scale=vs[:, g * P : (g + 1) * P],
                    rhs=hw[:, g, h * 1024 : (h + 1) * 1024].bitcast(FP4X4), rhs_scale=hs[:, g, h * KP : (h + 1) * KP],
                    start=(g == 0), stop=(g == GS - 1),
                )
            st["y", i, h] = y_ps

        def innovation(i, h):
            if h == 0:
                st["d", i] = work.tile([P, O], F32, name="d", bufs=2)
            cols = slice(h * KP, (h + 1) * KP)
            nc.vector.tensor_tensor(
                out=st["d", i][:, cols], in0=st["zb", i, h][:], in1=st["y", i, h][:], op=ALU.subtract
            )

        def whiten(i):
            u = work.tile([P, O], F32, name="u", bufs=2)
            nc.vector.tensor_tensor(out=u[:], in0=st["d", i][:], in1=chan[:, O : 2 * O], op=ALU.mult)
            st["u", i] = u

        def surprise(i):
            junk = work.tile([P, O], BF16, name="junk", bufs=1)
            nc.scalar.activation(out=junk[:], in_=st["u", i][:], func=ACT.Square, accum_out=ssq[:, i : i + 1])

        def weight_denominator(i):
            nc.scalar.activation(
                out=wden[:, i, 0:1], in_=ssq[:, i : i + 1], func=ACT.Copy, scale=1.0 / (O * (NU + 1.0)), bias=NU / (NU + 1.0)
            )

        def weight(i):
            nc.vector.reciprocal(out=wgt[:, i, 0:1], in_=wden[:, i, 0:1])
            if i == NT - 1:
                nt_ps = psum.tile([P, P], F32, name="nt_ps", tag="y0", bufs=1)
                nc.tensor.transpose(nt_ps[:], ssq[:], ident_f[:])
                nc.scalar.activation(out=nis_t[:], in_=nt_ps[0:NT, :], func=ACT.Copy, scale=1.0 / O)
                nc.scalar.dma_start(out=out_1.rearrange("(i m) o -> i (m o)", m=P), in_=nis_t[:])

        def clip(i):
            cl = work.tile([P, O], F32, name="cl", bufs=1)
            nc.vector.tensor_scalar(out=cl[:], in0=st["u", i][:], scalar1=-CLIP, scalar2=CLIP, op0=ALU.max, op1=ALU.min)
            st["cl", i] = cl

        def times_trust(i):
            e_sb = work.tile([P, O], BF16, name="e_sb", bufs=2)
            nc.vector.tensor_tensor(out=e_sb[:], in0=st["cl", i][:], in1=chan[:, 2 * O : 3 * O], op=ALU.mult)
            st["e", i] = e_sb

        def e_transposes(i):
            et_ps = psum.tile([P, KP], F32, name="et_ps", tag="et", bufs=1)
            words = st["e", i][:].bitcast(F32)
            for k in range(4):
                h, u = k // 2, k % 2
                nc.tensor.transpose(et_ps[:, k * P : (k + 1) * P], words[:, 256 * h + u : 256 * (h + 1) : 2], ident_f[:])
            st["et", i] = et_ps

        def e_copy(i):
            ei = work.tile([P, O], BF16, name="ei", bufs=2, align_bytes=64)
            nc.scalar.copy(
                out=ei[:].bitcast(F32).rearrange("p (h m u) -> p h m u", h=2, u=2),
                in_=st["et", i][:].rearrange("p (h u m) -> p h m u", h=2, u=2),
            )
            st["ei", i] = ei

        def e_quantize(i):
            eq = work.tile([P, 2 * P], U32, name="eq", bufs=2, align_bytes=64)
            es = work.tile([P, 2 * P], U8, name="es", bufs=2, align_bytes=64)
            nc.vector.quantize_mx(out=eq[:].bitcast(FP8X4), scales=es[:], in_=st["ei", i][:])
            st["eq", i] = (eq, es)

        def update_matmul(i, c):
            eq, es = st["eq", i]
            c_ps = psum.tile([P, KP], F32, name="c_ps", tag="acc", bufs=3)
            for h in range(GO):
                nc.tensor.matmul_mx(
                    out=c_ps[:],
                    lhsT=eq[:, h * P : (h + 1) * P].bitcast(FP8X4), lhsT_scale=es[:, h * P : (h + 1) * P],
                    rhs=gw[:, h, c * 2048 : (c + 1) * 2048].bitcast(FP8X4), rhs_scale=gs[:, h, c * KP : (c + 1) * KP],
                    start=(h == 0), stop=(h == GO - 1),
                )
            st["c", i, c] = c_ps

        def update_add(i, c):
            if c == 0:
                st["out", i] = work.tile([P, S], F32, name="out_sb", bufs=3)
            out_sb = st["out", i]
            cols = slice(c * KP, (c + 1) * KP)
            nc.vector.scalar_tensor_tensor(
                out=out_sb[:, cols], in0=st["c", i, c][:], scalar=wgt[:, i, 0:1], in1=st["xf", i, c][:],
                op0=ALU.mult, op1=ALU.add,
            )
            if i == NT - 1:
                last = out_sb[:, (c + 1) * KP - 4 : (c + 1) * KP]
                nc.gpsimd.tensor_tensor(out=last, in0=last, in1=xfix[:, i, c, :], op=ALU.add)
                nc.sync.dma_start(out=out_0[i * P : (i + 1) * P, cols], in_=out_sb[:, cols])
            elif c % 2 == 1:
                half = slice((c - 1) * KP, (c + 1) * KP)
                last = out_sb[:, half].rearrange("p (g r) -> p g r", g=2)[:, :, KP - 4 : KP]
                nc.gpsimd.tensor_tensor(out=last, in0=last, in1=xfix[:, i, c - 1 : c + 1, :], op=ALU.add)
                nc.sync.dma_start(out=out_0[i * P : (i + 1) * P, half], in_=out_sb[:, half])
        order = (
            (2, observe, (0,)),
            (0, update_add, (1,)),
            (3, x_affine, (1,)),
            (2, observe, (1,)),
            (1, times_trust, ()),
            (1, surprise, ()),
            (0, update_matmul, (3,)),
            (2, innovation, (0,)),
            (1, xf_products, (1,)),
            (3, x_interleave, ()),
            (1, e_transposes, ()),
            (3, x_copy, (1,)),
            (1, weight_denominator, ()),
            (4, x_transposes, (0,)),
            (3, x_group_scalar, ()),
            (3, z_bias, (0,)),
            (3, fix_columns, ()),
            (0, update_add, (2,)),
            (1, e_copy, ()),
            (1, weight, ()),
            (0, update_add, (3,)),
            (2, xf_products, (0,)),
            (1, xf_copy, (1,)),
            (2, innovation, (1,)),
            (1, xf_products, (2,)),
            (2, xf_copy, (0,)),
            (1, xf_products, (3,)),
            (1, e_quantize, ()),
            (1, xf_copy, (2,)),
            (2, whiten, ()),
            (4, x_transposes, (1,)),
            (4, x_copy, (0,)),
            (1, update_matmul, (0,)),
            (1, xf_copy, (3,)),
            (3, x_quantize, ()),
            (1, update_matmul, (1,)),
            (4, x_affine, (0,)),
            (2, clip, ()),
            (1, update_matmul, (2,)),
            (3, z_bias, (1,)),
            (1, update_add, (0,)),
        )
        x_transposes(0, 0)
        x_transposes(0, 1)
        channel_matmuls()
        x_affine(0, 0)
        x_affine(0, 1)
        x_copy(0, 0)
        x_copy(0, 1)
        x_group_scalar(0)
        x_interleave(0)
        channel_copy(0, nc.scalar.copy)
        nc.scalar.copy(out=dec16[:].rearrange("p g r -> p (g r)"), in_=st["d16"][:])
        x_quantize(0)
        channel_copy(1, nc.vector.tensor_copy)
        channel_copy(2, nc.vector.tensor_copy)
        for g in range(GS):
            build_dmat(g)
        done = (x_transposes, x_affine, x_copy, x_group_scalar, x_interleave, x_quantize)
        for step in range(-4, NT):
            for lead, stage, args in order:
                if 0 <= step + lead < NT and not (step + lead == 0 and stage in done):
                    stage(step + lead, *args)
                if step + lead == 0 and stage is z_bias and args == (1,):
                    nc.gpsimd.memset(xts[2][:], 1.0)
                    nc.gpsimd.memset(ssq[:], 0.0)
